import numpy as np
import ml_dtypes


def mxq(x, axis, fmt="e4m3"):
    dtype, down = {"e4m3": (ml_dtypes.float8_e4m3fn, 7), "e5m2": (ml_dtypes.float8_e5m2, 14)}[fmt]
    v = np.moveaxis(np.asarray(x, np.float32).astype(ml_dtypes.bfloat16).astype(np.float64), axis, -1)
    blocks = v.reshape(v.shape[:-1] + (-1, 32))
    amax = np.abs(blocks).max(-1, keepdims=True)
    byte = np.maximum(np.where(amax > 0, np.frexp(amax)[1] - 1 + 127, 0) - down, 1)
    scale = np.exp2(byte - 127.0)
    codes = (blocks / scale).astype(np.float32).astype(dtype).astype(np.float64)
    return np.moveaxis((codes * scale).reshape(v.shape), -1, axis)


WIDE = False


def mx_kscale(k):
    if not WIDE:
        return np.ones(k)
    levels = np.array([10, -10, 5, -5, 0])
    if k % 512:
        return np.exp2(np.random.permutation(np.resize(levels, k // 32))).repeat(32)
    a = np.empty((k // 512, 16))
    for p in range(k // 512):
        a[p, :8] = np.random.permutation(np.resize(levels, 8))
        for g in range(8):
            far = levels[np.abs(levels - a[p, g]) >= 10]
            a[p, g + 8] = far[np.random.randint(len(far))]
    return np.exp2(a.ravel()).repeat(32)


def f64(x):
    return np.asarray(x).astype(np.float64)


def striped(idx):
    return np.tile(idx.reshape(-1, 16).T, (8, 1)).astype(np.uint16)


def unstriped(offs):
    return offs[:16].T.reshape(-1).astype(np.int64)


E2M1 = np.array([0.0, 0.5, 1.0, 1.5, 2.0, 3.0, 4.0, 6.0, -0.0, -0.5, -1.0, -1.5, -2.0, -3.0, -4.0, -6.0])


def pack_weight(w, fmt):
    k, n = w.shape
    w = f64(np.asarray(w, np.float32).astype(ml_dtypes.bfloat16)).reshape(k // 32, 32, n)
    amax = np.abs(w).max(1)
    if fmt == "e4m3":
        byte = np.frexp(amax)[1] - 1 + 127 - 7
    else:
        mant, ex = np.frexp(amax / 6.0)
        byte = np.where(mant > 0.5, ex, ex - 1) + 127
    byte = np.clip(np.where(amax > 0, byte, 1), 1, 254)
    scaled = (w * np.exp2(127.0 - byte)[:, None, :]).reshape(k, n).astype(np.float32)
    by_word = np.ascontiguousarray(scaled.reshape(k // 512, 128, 4, n).transpose(0, 1, 3, 2))
    if fmt == "e4m3":
        words = by_word.astype(ml_dtypes.float8_e4m3fn).view(np.uint8)
    else:
        c = by_word.astype(ml_dtypes.float4_e2m1fn).view(np.uint8) & 0xF
        words = (c[..., 0::2] | (c[..., 1::2] << 4)).reshape(k // 512, 128, 2 * n)
    return np.ascontiguousarray(words), np.ascontiguousarray(byte.astype(np.uint8).reshape(k // 512, 16, n))


def unpack_weight(words, scales, fmt):
    g, _, n = scales.shape
    words = np.ascontiguousarray(words).reshape(g, 128, n, -1)
    if fmt == "e4m3":
        vals = words.view(ml_dtypes.float8_e4m3fn).astype(np.float64)
    else:
        nib = np.empty((g, 128, n, 4), np.uint8)
        nib[..., 0::2] = words & 0xF
        nib[..., 1::2] = words >> 4
        vals = E2M1[nib]
    vals = vals * np.repeat(np.exp2(scales.astype(np.float64) - 127.0), 8, axis=1)[..., None]
    return vals.transpose(0, 1, 3, 2).reshape(g * 512, n)


def gelu(v):
    return 0.5 * v * (1.0 + np.tanh(np.sqrt(2.0 / np.pi) * (v + 0.044715 * v**3)))


K, K2, H, N, T, S = 1024, 512, 1024, 384, 4096, 1024


def setup_inputs():
    n = np.random.standard_normal
    s = mx_kscale(K)[:, None]
    s2 = mx_kscale(K2)[:, None]
    u = mx_kscale(H)[:, None]
    d = {}
    d["tab_words"], d["tab_scales"] = pack_weight(n((K, T)) * s, "e4m3")
    d["offs"] = striped(np.random.permutation(T)[:S])
    d["xs_words"], d["xs_scales"] = pack_weight(n((K2, S)) * s2, "e4m3")
    d["w1"] = (n((K, H)) / s / K**0.5).astype(np.float32)
    d["w2_words"], d["w2_scales"] = pack_weight(n((K2, H)) / s2 / K2**0.5, "e2m1")
    d["b1"] = (0.5 * n(H)).astype(np.float32)
    d["gain"] = (np.exp(0.3 * n(H)) * u[:, 0]).astype(np.float32)
    d["w3"] = (n((K2, N)) / s2 / K2**0.5).astype(np.float32)
    d["w4_words"], d["w4_scales"] = pack_weight(n((H, N)) / u / H**0.5, "e2m1")
    return d


def reference(tab_words, tab_scales, offs, xs_words, xs_scales, w1, w2_words, w2_scales, b1, gain, w3, w4_words, w4_scales):
    v = unpack_weight(tab_words, tab_scales, "e4m3")[:, unstriped(offs)]
    xs = unpack_weight(xs_words, xs_scales, "e4m3")
    w2 = unpack_weight(w2_words, w2_scales, "e2m1")
    w4 = unpack_weight(w4_words, w4_scales, "e2m1")
    p = (mxq(f64(w1), 0, "e4m3").T @ v + w2.T @ xs) + f64(b1)[:, None]
    h = p / (1.0 + np.exp(-p)) * f64(gain)[:, None]
    y = w4.T @ mxq(h, 0, "e4m3")
    skip = mxq(f64(w3), 0, "e4m3").T @ xs
    return y / (1.0 + np.abs(skip))

@@ -1,0 +1,294 @@
+from contextlib import ExitStack
+
+import concourse.mybir as mybir
+
+K, K2, H, N, T, S = 1024, 512, 1024, 384, 4096, 1024
+FLOPS = 2 * S * (K * H + K2 * H + H * N + K2 * N)
+
+F32 = mybir.dt.float32
+BF16 = mybir.dt.bfloat16
+I32 = mybir.dt.int32
+U32 = mybir.dt.uint32
+U16 = mybir.dt.uint16
+U8 = mybir.dt.uint8
+FP8X4 = mybir.dt.float8_e4m3fn_x4
+FP4X4 = mybir.dt.float4_e2m1fn_x4
+ACT = mybir.ActivationFunctionType
+MULT = mybir.AluOpType.mult
+
+P = 128
+PACK = 4
+PASS = P * PACK
+BANK = 512
+HALF = BANK // 2
+QUADS = 4
+RUN = 4
+
+
+def tile_list_pool_dosing_scores_kernel(
+    tc, tab_words, tab_scales, offs, xs_words, xs_scales, w1, w2_words, w2_scales, b1, gain, w3, w4_words, w4_scales, out
+):
+    nc = tc.nc
+    with ExitStack() as ctx:
+        keep = ctx.enter_context(tc.tile_pool(name="keep", bufs=1))
+        psum = ctx.enter_context(tc.psum_pool(name="psum", bufs=1))
+
+        def tile(name, shape, dtype):
+            return keep.tile([P] + shape, dtype, name=name, align_bytes=64)
+
+        def bank(name, index):
+            return psum.tile([P, BANK], F32, name=name, tag="bank%d" % index)
+
+        def load_scale_rows(queue, plane, first, rows):
+            for q in range(QUADS):
+                queue.dma_start(
+                    out=plane[32 * q + first : 32 * q + first + 4].bitcast(I32),
+                    in_=rows[4 * q : 4 * q + 4].bitcast(I32),
+                )
+
+        offsets = keep.tile([P, S // 16], U16, name="offsets")
+        xs_plane = tile("xs_plane", [S], U8)
+        tab_plane = tile("tab_plane", [T], U8)
+        w2_plane_raw = tile("w2_plane_raw", [H], U8)
+        w4_plane = tile("w4_plane", [H // PASS, N], U8)
+        nc.gpsimd.memset(tab_plane[:, : T // 2].bitcast(I32), 0)
+        nc.vector.memset(tab_plane[:, T // 2 :].bitcast(I32), 0)
+        for plane in (xs_plane, w2_plane_raw):
+            nc.vector.memset(plane[:].bitcast(I32), 0)
+        nc.vector.memset(w4_plane[:].rearrange("p a n -> p (a n)").bitcast(I32), 0)
+
+        load_scale_rows(nc.gpsimd, xs_plane, 0, xs_scales[0])
+        load_scale_rows(nc.gpsimd, w2_plane_raw, 0, w2_scales[0])
+        w3_raw = tile("w3_raw", [PACK, N], F32)
+        nc.sync.dma_start(out=w3_raw[:], in_=w3.rearrange("(p i) n -> p i n", i=PACK))
+        xs_codes = tile("xs_codes", [S], I32)
+        nc.sync.dma_start(out=xs_codes[:], in_=xs_words[0].rearrange("p c i -> p (c i)").bitcast(I32))
+        w2_raw = tile("w2_raw", [2 * H], U8)
+        nc.sync.dma_start(out=w2_raw[:].bitcast(I32), in_=w2_words[0].bitcast(I32))
+        nc.sync.dma_start(offsets[:], offs)
+        tab_codes = [tile("tab_codes%d" % a, [T], I32) for a in range(K // PASS)]
+        bias = tile("bias", [H // PASS, PACK], F32)
+        gains = tile("gains", [H // PASS, PACK], F32)
+        load_scale_rows(nc.sync, tab_plane, 0, tab_scales[0])
+        nc.sync.dma_start(out=tab_codes[0][:], in_=tab_words[0].rearrange("p c i -> p (c i)").bitcast(I32))
+        load_scale_rows(nc.sync, tab_plane, 4, tab_scales[1])
+        nc.sync.dma_start(out=bias[:], in_=b1.rearrange("(b p t) -> p b t", p=P, t=PACK))
+        nc.sync.dma_start(out=gains[:], in_=gain.rearrange("(b p t) -> p b t", p=P, t=PACK))
+        nc.sync.dma_start(out=tab_codes[1][:], in_=tab_words[1].rearrange("p c i -> p (c i)").bitcast(I32))
+
+        w1_raw = {}
+        for b in range(H // PASS):
+            for a in range(K // PASS):
+                widths = (HALF, HALF) if (b, a) == (0, 1) else (PASS,)
+                first = 0
+                w1_raw[b, a] = []
+                for width in widths:
+                    raw = tile("w1_raw%d%d_%d" % (b, a, first), [PACK, width], F32)
+                    rows = w1[a * PASS : (a + 1) * PASS, b * PASS + first : b * PASS + first + width]
+                    nc.sync.dma_start(out=raw[:], in_=rows.rearrange("(p i) r -> p i r", i=PACK))
+                    w1_raw[b, a].append((first, width, raw))
+                    first = first + width
+        w4_codes = tile("w4_codes", [H // PASS, 2 * N], U8)
+        nc.sync.dma_start(out=w4_codes[:].bitcast(I32), in_=w4_words.rearrange("b p c -> p b c").bitcast(I32))
+        load_scale_rows(nc.sync, w4_plane, 0, w4_scales.rearrange("b q n -> q b n"))
+
+        w3_bf = tile("w3_bf", [N * PACK], BF16)
+        nc.vector.tensor_copy(
+            out=w3_bf[:].rearrange("p (c u i) -> p c i u", u=RUN, i=PACK),
+            in_=w3_raw[:].rearrange("p i (c u) -> p c i u", u=RUN),
+        )
+        w3_codes = tile("w3_codes", [N], U32)
+        w3_plane = tile("w3_plane", [N], U8)
+        for lo, hi in ((0, P), (P, N)):
+            nc.vector.quantize_mx(
+                out=w3_codes[:, lo:hi].bitcast(FP8X4), scales=w3_plane[:, lo:hi], in_=w3_bf[:, PACK * lo : PACK * hi]
+            )
+        damp = {}
+        mags = {}
+        for nt in range(N // P):
+            mag = tile("mag%d" % nt, [S], F32)
+            for jh in range(S // BANK):
+                acc = bank("skip%d%d" % (nt, jh), 2 * nt + jh)
+                cols = slice(jh * BANK, (jh + 1) * BANK)
+                nc.tensor.matmul_mx(
+                    out=acc[:],
+                    lhsT=w3_codes[:, nt * P : (nt + 1) * P].bitcast(FP8X4),
+                    lhsT_scale=w3_plane[:, nt * P : (nt + 1) * P],
+                    rhs=xs_codes[:, cols].bitcast(FP8X4),
+                    rhs_scale=xs_plane[:, cols],
+                    start=True,
+                    stop=True,
+                )
+                nc.scalar.activation(mag[:, cols], acc[:], ACT.Abs)
+            mags[nt] = mag
+        for nt in range(N // P):
+            root = tile("root%d" % nt, [S], F32)
+            nc.scalar.activation(root[:], mags[nt][:], ACT.Abs_reciprocal_sqrt, bias=1.0)
+            damp[nt] = tile("damp%d" % nt, [S], F32)
+            nc.scalar.activation(damp[nt][:], root[:], ACT.Square)
+
+        w2_codes = tile("w2_codes", [2 * H], U8)
+        nc.vector.tensor_copy(
+            out=w2_codes[:].bitcast(U16).rearrange("p (b t m) -> p b t m", t=PACK, m=P),
+            in_=w2_raw[:].bitcast(U16).rearrange("p (b m t) -> p b t m", t=PACK, m=P),
+        )
+        w2_plane = tile("w2_plane", [H], U8)
+        nc.vector.tensor_copy(
+            out=w2_plane[:].rearrange("p (b t m) -> p b t m", t=PACK, m=P),
+            in_=w2_plane_raw[:].rearrange("p (b m t) -> p b t m", t=PACK, m=P),
+        )
+
+        v_codes = [tile("v_codes%d" % a, [S], U32) for a in range(K // PASS)]
+        v_plane = tile("v_plane", [S], U8)
+        nc.vector.tensor_copy(v_codes[0][:], tab_codes[0][:].bitcast(U32).indirect(offsets[:]))
+        nc.vector.tensor_copy(v_plane[:], tab_plane[:].indirect(offsets[:]))
+        nc.vector.tensor_copy(v_codes[1][:], tab_codes[1][:].bitcast(U32).indirect(offsets[:]))
+
+        w1_bf, w1_codes, w1_plane = {}, {}, {}
+
+        def cast_w1(b, a, engine_copy):
+            w1_bf[b, a] = tile("w1_bf%d%d" % (b, a), [PASS * PACK], BF16)
+            dealt = w1_bf[b, a][:].rearrange("p (t m i) -> p m i t", t=PACK, i=PACK)
+            for first, width, raw in w1_raw[b, a]:
+                engine_copy(
+                    out=dealt[:, first // PACK : (first + width) // PACK],
+                    in_=raw[:].rearrange("p i (m t) -> p m i t", t=PACK),
+                )
+
+        def quantize_w1(b, a, width):
+            w1_codes[b, a] = tile("w1_codes%d%d" % (b, a), [PASS], U32)
+            w1_plane[b, a] = tile("w1_plane%d%d" % (b, a), [PASS], U8)
+            for lo in range(0, PASS, width):
+                nc.vector.quantize_mx(
+                    out=w1_codes[b, a][:, lo : lo + width].bitcast(FP8X4),
+                    scales=w1_plane[b, a][:, lo : lo + width],
+                    in_=w1_bf[b, a][:, PACK * lo : PACK * (lo + width)],
+                )
+
+        pre = {}
+
+        def probe_pass(b, jh):
+            cols = slice(jh * BANK, (jh + 1) * BANK)
+            for t in range(PACK):
+                pre[b, jh, t] = bank("pre%d%d%d" % (b, jh, t), PACK * jh + t)
+                first = b * PASS + t * P
+                nc.tensor.matmul_mx(
+                    out=pre[b, jh, t][:],
+                    lhsT=w2_codes[:, 2 * first : 2 * (first + P)].bitcast(FP4X4),
+                    lhsT_scale=w2_plane[:, first : first + P],
+                    rhs=xs_codes[:, cols].bitcast(FP8X4),
+                    rhs_scale=xs_plane[:, cols],
+                    start=True,
+                    stop=False,
+                )
+
+        def table_pass(b, jh, a):
+            cols = slice(jh * BANK, (jh + 1) * BANK)
+            for t in range(PACK):
+                nc.tensor.matmul_mx(
+                    out=pre[b, jh, t][:],
+                    lhsT=w1_codes[b, a][:, t * P : (t + 1) * P].bitcast(FP8X4),
+                    lhsT_scale=w1_plane[b, a][:, t * P : (t + 1) * P],
+                    rhs=v_codes[a][:, cols].bitcast(FP8X4),
+                    rhs_scale=v_plane[4 * a : P, cols],
+                    start=False,
+                    stop=(a == K // PASS - 1),
+                )
+
+        act, h_bf, h_codes, h_plane = {}, {}, {}, {}
+
+        def silu(b, jh, half):
+            act[b, jh, half] = tile("act%d%d%d" % (b, jh, half), [PACK, HALF], F32)
+            for t in range(PACK):
+                nc.scalar.activation(
+                    act[b, jh, half][:, t, :],
+                    pre[b, jh, t][:, half * HALF : (half + 1) * HALF],
+                    ACT.Silu,
+                    bias=bias[:, b, t : t + 1],
+                )
+
+        def apply_gain(b, jh, half):
+            h_bf[b, jh, half] = tile("h_bf%d%d%d" % (b, jh, half), [HALF * PACK], BF16)
+            nc.vector.tensor_tensor(
+                out=h_bf[b, jh, half][:].rearrange("p (c u t) -> p c t u", u=RUN, t=PACK),
+                in0=act[b, jh, half][:].rearrange("p t (c u) -> p c t u", u=RUN),
+                in1=gains[:, b : b + 1, :].unsqueeze(3).to_broadcast([P, HALF // RUN, PACK, RUN]),
+                op=MULT,
+            )
+
+        def quantize_h(b, jh, half):
+            if half == 0:
+                h_codes[b, jh] = tile("h_codes%d%d" % (b, jh), [BANK], U32)
+                h_plane[b, jh] = tile("h_plane%d%d" % (b, jh), [BANK], U8)
+            cols = slice(half * HALF, (half + 1) * HALF)
+            nc.vector.quantize_mx(
+                out=h_codes[b, jh][:, cols].bitcast(FP8X4), scales=h_plane[b, jh][:, cols], in_=h_bf[b, jh, half][:]
+            )
+
+        scores = {}
+
+        def score_pass(jh, b):
+            for nt in range(N // P):
+                if b == 0:
+                    scores[jh, nt] = bank("score%d%d" % (jh, nt), PACK * jh + nt)
+                nc.tensor.matmul_mx(
+                    out=scores[jh, nt][:],
+                    lhsT=w4_codes[:, b, 2 * nt * P : 2 * (nt + 1) * P].bitcast(FP4X4),
+                    lhsT_scale=w4_plane[:, b, nt * P : (nt + 1) * P],
+                    rhs=h_codes[b, jh][:].bitcast(FP8X4),
+                    rhs_scale=h_plane[b, jh][:],
+                    start=(b == 0),
+                    stop=(b == H // PASS - 1),
+                )
+
+        def finish(jh):
+            cols = slice(jh * BANK, (jh + 1) * BANK)
+            for nt in range(N // P):
+                result = tile("result%d%d" % (jh, nt), [BANK], F32)
+                nc.vector.tensor_tensor(out=result[:], in0=scores[jh, nt][:], in1=damp[nt][:, cols], op=MULT)
+                nc.sync.dma_start(out=out[nt * P : (nt + 1) * P, cols], in_=result[:])
+
+        cast_w1(0, 0, nc.vector.tensor_copy)
+        probe_pass(0, 0)
+        probe_pass(0, 1)
+        quantize_w1(0, 0, PASS)
+        table_pass(0, 0, 0)
+        table_pass(0, 1, 0)
+        cast_w1(0, 1, nc.vector.tensor_copy)
+        quantize_w1(0, 1, P)
+        table_pass(0, 0, 1)
+        table_pass(0, 1, 1)
+
+        silu(0, 0, 0)
+        silu(0, 0, 1)
+        cast_w1(1, 0, nc.scalar.copy)
+        apply_gain(0, 0, 0)
+        apply_gain(0, 0, 1)
+        quantize_h(0, 0, 0)
+        cast_w1(1, 1, nc.vector.tensor_copy)
+        quantize_h(0, 0, 1)
+        quantize_w1(1, 0, PASS)
+        quantize_w1(1, 1, PASS)
+        probe_pass(1, 0)
+        table_pass(1, 0, 0)
+        table_pass(1, 0, 1)
+        silu(0, 1, 0)
+        silu(0, 1, 1)
+        probe_pass(1, 1)
+        table_pass(1, 1, 0)
+        table_pass(1, 1, 1)
+        silu(1, 0, 0)
+        silu(1, 0, 1)
+        silu(1, 1, 0)
+        silu(1, 1, 1)
+        steps = [(b, jh, half) for b, jh in ((0, 1), (1, 0), (1, 1)) for half in range(2)]
+        for i, step in enumerate(steps):
+            apply_gain(*step)
+            if i > 0:
+                quantize_h(*steps[i - 1])
+        quantize_h(*steps[-1])
+        for jh in range(S // BANK):
+            score_pass(jh, 0)
+            score_pass(jh, 1)
+        finish(0)
+        finish(1)

@@ -51,35 +51,47 @@ def tile_list_pool_dosing_scores_kernel(
         tab_plane = tile("tab_plane", [T], U8)
         w2_plane_raw = tile("w2_plane_raw", [H], U8)
         w4_plane = tile("w4_plane", [H // PASS, N], U8)
-        nc.gpsimd.memset(tab_plane[:, : T // 2].bitcast(I32), 0)
-        nc.vector.memset(tab_plane[:, T // 2 :].bitcast(I32), 0)
-        for plane in (xs_plane, w2_plane_raw):
+        nc.gpsimd.memset(xs_plane[:].bitcast(I32), 0)
+        for plane in (w2_plane_raw, tab_plane):
             nc.vector.memset(plane[:].bitcast(I32), 0)
         nc.vector.memset(w4_plane[:].rearrange("p a n -> p (a n)").bitcast(I32), 0)
 
-        load_scale_rows(nc.gpsimd, xs_plane, 0, xs_scales[0])
-        load_scale_rows(nc.gpsimd, w2_plane_raw, 0, w2_scales[0])
         w3_raw = tile("w3_raw", [PACK, N], F32)
-        nc.sync.dma_start(out=w3_raw[:], in_=w3.rearrange("(p i) n -> p i n", i=PACK))
         xs_codes = tile("xs_codes", [S], I32)
-        nc.sync.dma_start(out=xs_codes[:], in_=xs_words[0].rearrange("p c i -> p (c i)").bitcast(I32))
         w2_raw = tile("w2_raw", [2 * H], U8)
-        nc.sync.dma_start(out=w2_raw[:].bitcast(I32), in_=w2_words[0].bitcast(I32))
-        nc.sync.dma_start(offsets[:], offs)
         tab_codes = [tile("tab_codes%d" % a, [T], I32) for a in range(K // PASS)]
         bias = tile("bias", [H // PASS, PACK], F32)
         gains = tile("gains", [H // PASS, PACK], F32)
-        load_scale_rows(nc.sync, tab_plane, 0, tab_scales[0])
-        nc.sync.dma_start(out=tab_codes[0][:], in_=tab_words[0].rearrange("p c i -> p (c i)").bitcast(I32))
-        load_scale_rows(nc.sync, tab_plane, 4, tab_scales[1])
-        nc.sync.dma_start(out=bias[:], in_=b1.rearrange("(b p t) -> p b t", p=P, t=PACK))
-        nc.sync.dma_start(out=gains[:], in_=gain.rearrange("(b p t) -> p b t", p=P, t=PACK))
-        nc.sync.dma_start(out=tab_codes[1][:], in_=tab_words[1].rearrange("p c i -> p (c i)").bitcast(I32))
+
+        def load_table_half(a, half):
+            cols = slice(half * T // 2, (half + 1) * T // 2)
+            nc.sync.dma_start(out=tab_codes[a][:, cols], in_=tab_words[a].rearrange("p c i -> p (c i)").bitcast(I32)[:, cols])
+
+        def load_table_scales(quads):
+            for a, q in quads:
+                nc.sync.dma_start(
+                    out=tab_plane[32 * q + 4 * a : 32 * q + 4 * a + 4].bitcast(I32),
+                    in_=tab_scales[a, 4 * q : 4 * q + 4].bitcast(I32),
+                )
+
+        quads = [(a, q) for a in range(K // PASS) for q in range(QUADS)]
+        load_scale_rows(nc.sync, xs_plane, 0, xs_scales[0])
+        nc.sync.dma_start(out=w3_raw[:], in_=w3.rearrange("(p i) n -> p i n", i=PACK))
+        nc.sync.dma_start(out=xs_codes[:], in_=xs_words[0].rearrange("p c i -> p (c i)").bitcast(I32))
+        nc.sync.dma_start(out=w2_raw[:].bitcast(I32), in_=w2_words[0].bitcast(I32))
+        load_table_half(0, 0)
+        load_scale_rows(nc.sync, w2_plane_raw, 0, w2_scales[0])
+        load_table_half(0, 1)
+        nc.sync.dma_start(offsets[:], offs)
+        load_table_scales(quads[:5])
+        load_table_half(1, 0)
+        load_table_scales(quads[5:])
+        load_table_half(1, 1)
 
         w1_raw = {}
         for b in range(H // PASS):
             for a in range(K // PASS):
-                widths = (HALF, HALF) if (b, a) == (0, 1) else (PASS,)
+                widths = (HALF, HALF) if (b, a) in ((0, 1), (1, 0)) else (PASS,)
                 first = 0
                 w1_raw[b, a] = []
                 for width in widths:
@@ -88,6 +100,9 @@ def tile_list_pool_dosing_scores_kernel(
                     nc.sync.dma_start(out=raw[:], in_=rows.rearrange("(p i) r -> p i r", i=PACK))
                     w1_raw[b, a].append((first, width, raw))
                     first = first + width
+                if (b, a) == (0, 0):
+                    nc.sync.dma_start(out=bias[:], in_=b1.rearrange("(b p t) -> p b t", p=P, t=PACK))
+                    nc.sync.dma_start(out=gains[:], in_=gain.rearrange("(b p t) -> p b t", p=P, t=PACK))
         w4_codes = tile("w4_codes", [H // PASS, 2 * N], U8)
         nc.sync.dma_start(out=w4_codes[:].bitcast(I32), in_=w4_words.rearrange("b p c -> p b c").bitcast(I32))
         load_scale_rows(nc.sync, w4_plane, 0, w4_scales.rearrange("b q n -> q b n"))
@@ -261,31 +276,29 @@ def tile_list_pool_dosing_scores_kernel(
 
         silu(0, 0, 0)
         silu(0, 0, 1)
-        cast_w1(1, 0, nc.scalar.copy)
-        apply_gain(0, 0, 0)
-        apply_gain(0, 0, 1)
-        quantize_h(0, 0, 0)
-        cast_w1(1, 1, nc.vector.tensor_copy)
-        quantize_h(0, 0, 1)
-        quantize_w1(1, 0, PASS)
-        quantize_w1(1, 1, PASS)
-        probe_pass(1, 0)
-        table_pass(1, 0, 0)
-        table_pass(1, 0, 1)
         silu(0, 1, 0)
         silu(0, 1, 1)
+        cast_w1(1, 1, nc.scalar.copy)
+        cast_w1(1, 0, nc.vector.tensor_copy)
+        apply_gain(0, 0, 0)
+        quantize_w1(1, 0, PASS)
+        apply_gain(0, 0, 1)
+        quantize_h(0, 0, 0)
+        probe_pass(1, 0)
+        table_pass(1, 0, 0)
         probe_pass(1, 1)
         table_pass(1, 1, 0)
+        quantize_w1(1, 1, PASS)
+        table_pass(1, 0, 1)
         table_pass(1, 1, 1)
         silu(1, 0, 0)
         silu(1, 0, 1)
         silu(1, 1, 0)
         silu(1, 1, 1)
-        steps = [(b, jh, half) for b, jh in ((0, 1), (1, 0), (1, 1)) for half in range(2)]
-        for i, step in enumerate(steps):
-            apply_gain(*step)
-            if i > 0:
-                quantize_h(*steps[i - 1])
+        steps = [(0, 0, 1)] + [(b, jh, half) for b, jh in ((0, 1), (1, 0), (1, 1)) for half in range(2)]
+        for i in range(1, len(steps)):
+            apply_gain(*steps[i])
+            quantize_h(*steps[i - 1])
         quantize_h(*steps[-1])
         for jh in range(S // BANK):
             score_pass(jh, 0)

@@ -40,19 +40,17 @@ def tile_list_pool_dosing_scores_kernel(
             return psum.tile([P, BANK], F32, name=name, tag="bank%d" % index)
 
         def load_scale_rows(queue, plane, first, rows):
-            for q in range(QUADS):
-                queue.dma_start(
-                    out=plane[32 * q + first : 32 * q + first + 4].bitcast(I32),
-                    in_=rows[4 * q : 4 * q + 4].bitcast(I32),
-                )
+            for r in range(4):
+                queue.dma_start(out=plane[first + r : P : 32].bitcast(I32), in_=rows[r : 16 : 4].bitcast(I32))
 
         offsets = keep.tile([P, S // 16], U16, name="offsets")
         xs_plane = tile("xs_plane", [S], U8)
         tab_plane = tile("tab_plane", [T], U8)
+        v_plane = tile("v_plane", [S], U8)
         w2_plane_raw = tile("w2_plane_raw", [H], U8)
         w4_plane = tile("w4_plane", [H // PASS, N], U8)
         nc.gpsimd.memset(xs_plane[:].bitcast(I32), 0)
-        for plane in (w2_plane_raw, tab_plane):
+        for plane in (tab_plane, w2_plane_raw, v_plane):
             nc.vector.memset(plane[:].bitcast(I32), 0)
         nc.vector.memset(w4_plane[:].rearrange("p a n -> p (a n)").bitcast(I32), 0)
 
@@ -67,25 +65,16 @@ def tile_list_pool_dosing_scores_kernel(
             cols = slice(half * T // 2, (half + 1) * T // 2)
             nc.sync.dma_start(out=tab_codes[a][:, cols], in_=tab_words[a].rearrange("p c i -> p (c i)").bitcast(I32)[:, cols])
 
-        def load_table_scales(quads):
-            for a, q in quads:
-                nc.sync.dma_start(
-                    out=tab_plane[32 * q + 4 * a : 32 * q + 4 * a + 4].bitcast(I32),
-                    in_=tab_scales[a, 4 * q : 4 * q + 4].bitcast(I32),
-                )
-
-        quads = [(a, q) for a in range(K // PASS) for q in range(QUADS)]
         load_scale_rows(nc.sync, xs_plane, 0, xs_scales[0])
         nc.sync.dma_start(out=w3_raw[:], in_=w3.rearrange("(p i) n -> p i n", i=PACK))
         nc.sync.dma_start(out=xs_codes[:], in_=xs_words[0].rearrange("p c i -> p (c i)").bitcast(I32))
-        nc.sync.dma_start(out=w2_raw[:].bitcast(I32), in_=w2_words[0].bitcast(I32))
+        nc.sync.dma_start(out=tab_plane[0:P:4].bitcast(I32), in_=tab_scales.rearrange("a q c -> (a q) c").bitcast(I32))
+        nc.sync.dma_start(offsets[:], offs)
         load_table_half(0, 0)
+        nc.sync.dma_start(out=w2_raw[:].bitcast(I32), in_=w2_words[0].bitcast(I32))
         load_scale_rows(nc.sync, w2_plane_raw, 0, w2_scales[0])
         load_table_half(0, 1)
-        nc.sync.dma_start(offsets[:], offs)
-        load_table_scales(quads[:5])
         load_table_half(1, 0)
-        load_table_scales(quads[5:])
         load_table_half(1, 1)
 
         w1_raw = {}
@@ -142,6 +131,11 @@ def tile_list_pool_dosing_scores_kernel(
             damp[nt] = tile("damp%d" % nt, [S], F32)
             nc.scalar.activation(damp[nt][:], root[:], ACT.Square)
 
+        v_rows = tile("v_rows", [S], U8)
+        nc.vector.tensor_copy(v_rows[:], tab_plane[:].indirect(offsets[:]))
+        for a in range(K // PASS):
+            load_scale_rows(nc.gpsimd, v_plane, 4 * a, v_rows[64 * a : 64 * (a + 1) : 4])
+
         w2_codes = tile("w2_codes", [2 * H], U8)
         nc.vector.tensor_copy(
             out=w2_codes[:].bitcast(U16).rearrange("p (b t m) -> p b t m", t=PACK, m=P),
@@ -154,9 +148,7 @@ def tile_list_pool_dosing_scores_kernel(
         )
 
         v_codes = [tile("v_codes%d" % a, [S], U32) for a in range(K // PASS)]
-        v_plane = tile("v_plane", [S], U8)
         nc.vector.tensor_copy(v_codes[0][:], tab_codes[0][:].bitcast(U32).indirect(offsets[:]))
-        nc.vector.tensor_copy(v_plane[:], tab_plane[:].indirect(offsets[:]))
         nc.vector.tensor_copy(v_codes[1][:], tab_codes[1][:].bitcast(U32).indirect(offsets[:]))
 
         w1_bf, w1_codes, w1_plane = {}, {}, {}

@@ -19,10 +19,13 @@ MULT = mybir.AluOpType.mult
 P = 128
 PACK = 4
 PASS = P * PACK
+BLOCKS = PASS // 32
+QUADRANT = 32
+LIVE = 4
 BANK = 512
 HALF = BANK // 2
-QUADS = 4
-RUN = 4
+RUN = 2
+SPREAD = P // (2 * BLOCKS)
 
 
 def tile_list_pool_dosing_scores_kernel(
@@ -31,70 +34,57 @@ def tile_list_pool_dosing_scores_kernel(
     nc = tc.nc
     with ExitStack() as ctx:
         keep = ctx.enter_context(tc.tile_pool(name="keep", bufs=1))
+        late = ctx.enter_context(tc.tile_pool(name="late", bufs=1))
         psum = ctx.enter_context(tc.psum_pool(name="psum", bufs=1))
 
         def tile(name, shape, dtype):
             return keep.tile([P] + shape, dtype, name=name, align_bytes=64)
 
+        def placed(name, shape, dtype, offset):
+            return late.tile([P] + shape, dtype, name=name, align_bytes=64, offset=offset)
+
         def bank(name, index):
             return psum.tile([P, BANK], F32, name=name, tag="bank%d" % index)
 
-        def load_scale_rows(queue, plane, first, rows):
-            for r in range(4):
-                queue.dma_start(out=plane[first + r : P : 32].bitcast(I32), in_=rows[r : 16 : 4].bitcast(I32))
+        def load_plane(plane, rows):
+            for r in range(LIVE):
+                nc.sync.dma_start(out=plane[r:P:QUADRANT].bitcast(I32), in_=rows[r:BLOCKS:LIVE].bitcast(I32))
+
+        bias_at = 4 * T
+        gains_at = bias_at + 64
+        w4_codes_at = gains_at + 64
+        w4_plane_at = w4_codes_at + 4 * N
+        w1_at = w4_plane_at + 2 * N
+        tab_rows_at = bias_at - 1024
 
         offsets = keep.tile([P, S // 16], U16, name="offsets")
         xs_plane = tile("xs_plane", [S], U8)
-        tab_plane = tile("tab_plane", [T], U8)
-        v_plane = tile("v_plane", [S], U8)
+        tab_rows = placed("tab_rows", [T], U8, tab_rows_at)
+        v_plane = [tile("v_plane%d" % a, [S], U8) for a in range(K // PASS)]
         w2_plane_raw = tile("w2_plane_raw", [H], U8)
-        w4_plane = tile("w4_plane", [H // PASS, N], U8)
         nc.gpsimd.memset(xs_plane[:].bitcast(I32), 0)
-        for plane in (tab_plane, w2_plane_raw, v_plane):
-            nc.vector.memset(plane[:].bitcast(I32), 0)
-        nc.vector.memset(w4_plane[:].rearrange("p a n -> p (a n)").bitcast(I32), 0)
+        for zeroed in [tab_rows, w2_plane_raw] + v_plane:
+            nc.vector.memset(zeroed[:].bitcast(I32), 0)
 
         w3_raw = tile("w3_raw", [PACK, N], F32)
         xs_codes = tile("xs_codes", [S], I32)
         w2_raw = tile("w2_raw", [2 * H], U8)
-        tab_codes = [tile("tab_codes%d" % a, [T], I32) for a in range(K // PASS)]
-        bias = tile("bias", [H // PASS, PACK], F32)
-        gains = tile("gains", [H // PASS, PACK], F32)
+        tab_codes = [tile("tab_codes0", [T], I32), placed("tab_codes1", [T], I32, 0)]
 
         def load_table_half(a, half):
             cols = slice(half * T // 2, (half + 1) * T // 2)
-            nc.sync.dma_start(out=tab_codes[a][:, cols], in_=tab_words[a].rearrange("p c i -> p (c i)").bitcast(I32)[:, cols])
+            words = tab_words[a].rearrange("p c i -> p (c i)").bitcast(I32)
+            nc.sync.dma_start(out=tab_codes[a][:, cols], in_=words[:, cols])
 
-        load_scale_rows(nc.sync, xs_plane, 0, xs_scales[0])
+        load_plane(xs_plane, xs_scales[0])
         nc.sync.dma_start(out=w3_raw[:], in_=w3.rearrange("(p i) n -> p i n", i=PACK))
         nc.sync.dma_start(out=xs_codes[:], in_=xs_words[0].rearrange("p c i -> p (c i)").bitcast(I32))
-        nc.sync.dma_start(out=tab_plane[0:P:4].bitcast(I32), in_=tab_scales.rearrange("a q c -> (a q) c").bitcast(I32))
+        nc.sync.dma_start(out=tab_rows[0:P:SPREAD].bitcast(I32), in_=tab_scales.rearrange("a q c -> (a q) c").bitcast(I32))
         nc.sync.dma_start(offsets[:], offs)
         load_table_half(0, 0)
         nc.sync.dma_start(out=w2_raw[:].bitcast(I32), in_=w2_words[0].bitcast(I32))
-        load_scale_rows(nc.sync, w2_plane_raw, 0, w2_scales[0])
+        load_plane(w2_plane_raw, w2_scales[0])
         load_table_half(0, 1)
-        load_table_half(1, 0)
-        load_table_half(1, 1)
-
-        w1_raw = {}
-        for b in range(H // PASS):
-            for a in range(K // PASS):
-                widths = (HALF, HALF) if (b, a) in ((0, 1), (1, 0)) else (PASS,)
-                first = 0
-                w1_raw[b, a] = []
-                for width in widths:
-                    raw = tile("w1_raw%d%d_%d" % (b, a, first), [PACK, width], F32)
-                    rows = w1[a * PASS : (a + 1) * PASS, b * PASS + first : b * PASS + first + width]
-                    nc.sync.dma_start(out=raw[:], in_=rows.rearrange("(p i) r -> p i r", i=PACK))
-                    w1_raw[b, a].append((first, width, raw))
-                    first = first + width
-                if (b, a) == (0, 0):
-                    nc.sync.dma_start(out=bias[:], in_=b1.rearrange("(b p t) -> p b t", p=P, t=PACK))
-                    nc.sync.dma_start(out=gains[:], in_=gain.rearrange("(b p t) -> p b t", p=P, t=PACK))
-        w4_codes = tile("w4_codes", [H // PASS, 2 * N], U8)
-        nc.sync.dma_start(out=w4_codes[:].bitcast(I32), in_=w4_words.rearrange("b p c -> p b c").bitcast(I32))
-        load_scale_rows(nc.sync, w4_plane, 0, w4_scales.rearrange("b q n -> q b n"))
 
         w3_bf = tile("w3_bf", [N * PACK], BF16)
         nc.vector.tensor_copy(
@@ -107,15 +97,14 @@ def tile_list_pool_dosing_scores_kernel(
             nc.vector.quantize_mx(
                 out=w3_codes[:, lo:hi].bitcast(FP8X4), scales=w3_plane[:, lo:hi], in_=w3_bf[:, PACK * lo : PACK * hi]
             )
-        damp = {}
-        mags = {}
+        skip_abs = []
         for nt in range(N // P):
-            mag = tile("mag%d" % nt, [S], F32)
+            skip_abs.append(tile("skip_abs%d" % nt, [S], F32))
             for jh in range(S // BANK):
-                acc = bank("skip%d%d" % (nt, jh), 2 * nt + jh)
+                skip = bank("skip%d%d" % (nt, jh), 2 * nt + jh)
                 cols = slice(jh * BANK, (jh + 1) * BANK)
                 nc.tensor.matmul_mx(
-                    out=acc[:],
+                    out=skip[:],
                     lhsT=w3_codes[:, nt * P : (nt + 1) * P].bitcast(FP8X4),
                     lhsT_scale=w3_plane[:, nt * P : (nt + 1) * P],
                     rhs=xs_codes[:, cols].bitcast(FP8X4),
@@ -123,18 +112,51 @@ def tile_list_pool_dosing_scores_kernel(
                     start=True,
                     stop=True,
                 )
-                nc.scalar.activation(mag[:, cols], acc[:], ACT.Abs)
-            mags[nt] = mag
+                nc.scalar.activation(skip_abs[nt][:, cols], skip[:], ACT.Abs)
+        damp = []
         for nt in range(N // P):
             root = tile("root%d" % nt, [S], F32)
-            nc.scalar.activation(root[:], mags[nt][:], ACT.Abs_reciprocal_sqrt, bias=1.0)
-            damp[nt] = tile("damp%d" % nt, [S], F32)
+            nc.scalar.activation(root[:], skip_abs[nt][:], ACT.Abs_reciprocal_sqrt, bias=1.0)
+            damp.append(tile("damp%d" % nt, [S], F32))
             nc.scalar.activation(damp[nt][:], root[:], ACT.Square)
 
         v_rows = tile("v_rows", [S], U8)
-        nc.vector.tensor_copy(v_rows[:], tab_plane[:].indirect(offsets[:]))
-        for a in range(K // PASS):
-            load_scale_rows(nc.gpsimd, v_plane, 4 * a, v_rows[64 * a : 64 * (a + 1) : 4])
+        nc.vector.tensor_copy(v_rows[:], tab_rows[:].indirect(offsets[:]))
+
+        def move_scale_rows(a):
+            first = SPREAD * BLOCKS * a
+            for r in range(LIVE):
+                nc.sync.dma_start(
+                    out=v_plane[a][r:P:QUADRANT].bitcast(I32),
+                    in_=v_rows[first + SPREAD * r : first + SPREAD * BLOCKS : SPREAD * LIVE].bitcast(I32),
+                )
+
+        bias = placed("bias", [H // PASS, PACK], F32, bias_at)
+        gains = placed("gains", [H // PASS, PACK], F32, gains_at)
+        w4_codes = placed("w4_codes", [H // PASS, 2 * N], U8, w4_codes_at)
+        w4_plane = placed("w4_plane", [H // PASS, N], U8, w4_plane_at)
+        w1_all = placed("w1_all", [K * H // P], F32, w1_at)
+        nc.vector.memset(w4_plane[:].rearrange("p b n -> p (b n)").bitcast(I32), 0)
+        w1_raw = {}
+
+        def load_w1(b, a):
+            at = PACK * PASS * (2 * b + a)
+            w1_raw[b, a] = w1_all[:, at : at + PACK * PASS].rearrange("p (i c) -> p i c", i=PACK)
+            rows = w1[a * PASS : (a + 1) * PASS, b * PASS : (b + 1) * PASS]
+            nc.sync.dma_start(out=w1_raw[b, a], in_=rows.rearrange("(p i) c -> p i c", i=PACK))
+
+        move_scale_rows(0)
+        load_w1(0, 0)
+        load_table_half(1, 0)
+        load_table_half(1, 1)
+        load_w1(0, 1)
+        move_scale_rows(1)
+        nc.sync.dma_start(out=bias[:], in_=b1.rearrange("(b p t) -> p b t", p=P, t=PACK))
+        nc.sync.dma_start(out=gains[:], in_=gain.rearrange("(b p t) -> p b t", p=P, t=PACK))
+        load_w1(1, 0)
+        load_w1(1, 1)
+        nc.sync.dma_start(out=w4_codes[:].bitcast(I32), in_=w4_words.rearrange("b p c -> p b c").bitcast(I32))
+        load_plane(w4_plane, w4_scales.rearrange("b q n -> q b n"))
 
         w2_codes = tile("w2_codes", [2 * H], U8)
         nc.vector.tensor_copy(
@@ -148,36 +170,42 @@ def tile_list_pool_dosing_scores_kernel(
         )
 
         v_codes = [tile("v_codes%d" % a, [S], U32) for a in range(K // PASS)]
-        nc.vector.tensor_copy(v_codes[0][:], tab_codes[0][:].bitcast(U32).indirect(offsets[:]))
-        nc.vector.tensor_copy(v_codes[1][:], tab_codes[1][:].bitcast(U32).indirect(offsets[:]))
+
+        def gather_words(a):
+            nc.vector.tensor_copy(v_codes[a][:], tab_codes[a][:].bitcast(U32).indirect(offsets[:]))
+
+        gather_words(0)
 
         w1_bf, w1_codes, w1_plane = {}, {}, {}
+        for b in range(H // PASS):
+            for a in range(K // PASS):
+                w1_bf[b, a] = tile("w1_bf%d%d" % (b, a), [PASS * PACK], BF16)
+                w1_codes[b, a] = tile("w1_codes%d%d" % (b, a), [PASS], U32)
+                w1_plane[b, a] = tile("w1_plane%d%d" % (b, a), [PASS], U8)
 
-        def cast_w1(b, a, engine_copy):
-            w1_bf[b, a] = tile("w1_bf%d%d" % (b, a), [PASS * PACK], BF16)
-            dealt = w1_bf[b, a][:].rearrange("p (t m i) -> p m i t", t=PACK, i=PACK)
-            for first, width, raw in w1_raw[b, a]:
-                engine_copy(
-                    out=dealt[:, first // PACK : (first + width) // PACK],
-                    in_=raw[:].rearrange("p i (m t) -> p m i t", t=PACK),
-                )
+        def cast_w1(b, a, engine_copy, ts=slice(0, PACK), ms=slice(0, P)):
+            engine_copy(
+                out=w1_bf[b, a][:].rearrange("p (t m i) -> p m i t", t=PACK, i=PACK)[:, ms, :, ts],
+                in_=w1_raw[b, a].rearrange("p i (m t) -> p m i t", t=PACK)[:, ms, :, ts],
+            )
 
-        def quantize_w1(b, a, width):
-            w1_codes[b, a] = tile("w1_codes%d%d" % (b, a), [PASS], U32)
-            w1_plane[b, a] = tile("w1_plane%d%d" % (b, a), [PASS], U8)
-            for lo in range(0, PASS, width):
-                nc.vector.quantize_mx(
-                    out=w1_codes[b, a][:, lo : lo + width].bitcast(FP8X4),
-                    scales=w1_plane[b, a][:, lo : lo + width],
-                    in_=w1_bf[b, a][:, PACK * lo : PACK * (lo + width)],
-                )
+        def quantize_w1(b, a, first=0, last=PACK):
+            cols = slice(first * P, last * P)
+            nc.vector.quantize_mx(
+                out=w1_codes[b, a][:, cols].bitcast(FP8X4),
+                scales=w1_plane[b, a][:, cols],
+                in_=w1_bf[b, a][:, PACK * first * P : PACK * last * P],
+            )
 
         pre = {}
 
-        def probe_pass(b, jh):
-            cols = slice(jh * BANK, (jh + 1) * BANK)
+        def open_banks(b, jh):
             for t in range(PACK):
                 pre[b, jh, t] = bank("pre%d%d%d" % (b, jh, t), PACK * jh + t)
+
+        def probe_pass(b, jh, start):
+            cols = slice(jh * BANK, (jh + 1) * BANK)
+            for t in range(PACK):
                 first = b * PASS + t * P
                 nc.tensor.matmul_mx(
                     out=pre[b, jh, t][:],
@@ -185,11 +213,11 @@ def tile_list_pool_dosing_scores_kernel(
                     lhsT_scale=w2_plane[:, first : first + P],
                     rhs=xs_codes[:, cols].bitcast(FP8X4),
                     rhs_scale=xs_plane[:, cols],
-                    start=True,
+                    start=start,
                     stop=False,
                 )
 
-        def table_pass(b, jh, a):
+        def table_pass(b, jh, a, start=False):
             cols = slice(jh * BANK, (jh + 1) * BANK)
             for t in range(PACK):
                 nc.tensor.matmul_mx(
@@ -197,22 +225,23 @@ def tile_list_pool_dosing_scores_kernel(
                     lhsT=w1_codes[b, a][:, t * P : (t + 1) * P].bitcast(FP8X4),
                     lhsT_scale=w1_plane[b, a][:, t * P : (t + 1) * P],
                     rhs=v_codes[a][:, cols].bitcast(FP8X4),
-                    rhs_scale=v_plane[4 * a : P, cols],
-                    start=False,
+                    rhs_scale=v_plane[a][:, cols],
+                    start=start,
                     stop=(a == K // PASS - 1),
                 )
 
         act, h_bf, h_codes, h_plane = {}, {}, {}, {}
 
-        def silu(b, jh, half):
-            act[b, jh, half] = tile("act%d%d%d" % (b, jh, half), [PACK, HALF], F32)
-            for t in range(PACK):
-                nc.scalar.activation(
-                    act[b, jh, half][:, t, :],
-                    pre[b, jh, t][:, half * HALF : (half + 1) * HALF],
-                    ACT.Silu,
-                    bias=bias[:, b, t : t + 1],
-                )
+        def silu(b, jh):
+            for half in range(BANK // HALF):
+                act[b, jh, half] = tile("act%d%d%d" % (b, jh, half), [PACK, HALF], F32)
+                for t in range(PACK):
+                    nc.scalar.activation(
+                        act[b, jh, half][:, t, :],
+                        pre[b, jh, t][:, half * HALF : (half + 1) * HALF],
+                        ACT.Silu,
+                        bias=bias[:, b, t : t + 1],
+                    )
 
         def apply_gain(b, jh, half):
             h_bf[b, jh, half] = tile("h_bf%d%d%d" % (b, jh, half), [HALF * PACK], BF16)
@@ -248,52 +277,59 @@ def tile_list_pool_dosing_scores_kernel(
                     stop=(b == H // PASS - 1),
                 )
 
-        def finish(jh):
-            cols = slice(jh * BANK, (jh + 1) * BANK)
-            for nt in range(N // P):
-                result = tile("result%d%d" % (jh, nt), [BANK], F32)
-                nc.vector.tensor_tensor(out=result[:], in0=scores[jh, nt][:], in1=damp[nt][:, cols], op=MULT)
-                nc.sync.dma_start(out=out[nt * P : (nt + 1) * P, cols], in_=result[:])
+        def finish(jh, nt, first, width):
+            cols = slice(jh * BANK + first, jh * BANK + first + width)
+            result = tile("result%d%d_%d" % (jh, nt, first), [width], F32)
+            nc.vector.tensor_tensor(
+                out=result[:], in0=scores[jh, nt][:, first : first + width], in1=damp[nt][:, cols], op=MULT
+            )
+            nc.sync.dma_start(out=out[nt * P : (nt + 1) * P, cols], in_=result[:])
 
         cast_w1(0, 0, nc.vector.tensor_copy)
-        probe_pass(0, 0)
-        probe_pass(0, 1)
-        quantize_w1(0, 0, PASS)
-        table_pass(0, 0, 0)
-        table_pass(0, 1, 0)
-        cast_w1(0, 1, nc.vector.tensor_copy)
-        quantize_w1(0, 1, P)
+        quantize_w1(0, 0)
+        for jh in range(S // BANK):
+            open_banks(0, jh)
+            table_pass(0, jh, 0, start=True)
+        for jh in range(S // BANK):
+            probe_pass(0, jh, False)
+        gather_words(1)
+        for first in (0, 2):
+            cast_w1(0, 1, nc.vector.tensor_copy, ts=slice(first, first + 2))
+            quantize_w1(0, 1, first, first + 1)
+            quantize_w1(0, 1, first + 1, first + 2)
         table_pass(0, 0, 1)
         table_pass(0, 1, 1)
+        silu(0, 0)
+        silu(0, 1)
 
-        silu(0, 0, 0)
-        silu(0, 0, 1)
-        silu(0, 1, 0)
-        silu(0, 1, 1)
-        cast_w1(1, 1, nc.scalar.copy)
+        cast_w1(1, 1, nc.scalar.copy, ms=slice(0, P // 2))
         cast_w1(1, 0, nc.vector.tensor_copy)
         apply_gain(0, 0, 0)
-        quantize_w1(1, 0, PASS)
+        quantize_w1(1, 0)
         apply_gain(0, 0, 1)
+        cast_w1(1, 1, nc.vector.tensor_copy, ms=slice(P // 2, P))
         quantize_h(0, 0, 0)
-        probe_pass(1, 0)
-        table_pass(1, 0, 0)
-        probe_pass(1, 1)
-        table_pass(1, 1, 0)
-        quantize_w1(1, 1, PASS)
+        for jh in range(S // BANK):
+            open_banks(1, jh)
+            probe_pass(1, jh, True)
+            table_pass(1, jh, 0)
+        quantize_w1(1, 1)
         table_pass(1, 0, 1)
         table_pass(1, 1, 1)
-        silu(1, 0, 0)
-        silu(1, 0, 1)
-        silu(1, 1, 0)
-        silu(1, 1, 1)
-        steps = [(0, 0, 1)] + [(b, jh, half) for b, jh in ((0, 1), (1, 0), (1, 1)) for half in range(2)]
+        silu(1, 0)
+        silu(1, 1)
+
+        steps = [(0, 0, 1)] + [(b, jh, half) for b, jh in ((0, 1), (1, 0), (1, 1)) for half in range(BANK // HALF)]
         for i in range(1, len(steps)):
             apply_gain(*steps[i])
             quantize_h(*steps[i - 1])
         quantize_h(*steps[-1])
+
         for jh in range(S // BANK):
-            score_pass(jh, 0)
-            score_pass(jh, 1)
-        finish(0)
-        finish(1)
+            for b in range(H // PASS):
+                score_pass(jh, b)
+        tiles = [(jh, nt) for jh in range(S // BANK) for nt in range(N // P)]
+        for jh, nt in tiles[:-1]:
+            finish(jh, nt, 0, BANK)
+        for first in (0, HALF):
+            finish(*tiles[-1], first, HALF)

from contextlib import ExitStack

import concourse.mybir as mybir

K, K2, H, N, T, S = 1024, 512, 1024, 384, 4096, 1024
FLOPS = 2 * S * (K * H + K2 * H + H * N + K2 * N)

F32 = mybir.dt.float32
BF16 = mybir.dt.bfloat16
I32 = mybir.dt.int32
U32 = mybir.dt.uint32
U16 = mybir.dt.uint16
U8 = mybir.dt.uint8
FP8X4 = mybir.dt.float8_e4m3fn_x4
FP4X4 = mybir.dt.float4_e2m1fn_x4
ACT = mybir.ActivationFunctionType
MULT = mybir.AluOpType.mult

P = 128
PACK = 4
PASS = P * PACK
BLOCKS = PASS // 32
QUADRANT = 32
LIVE = 4
BANK = 512
HALF = BANK // 2
RUN = 2
SPREAD = P // (2 * BLOCKS)


def tile_list_pool_dosing_scores_kernel(
    tc, tab_words, tab_scales, offs, xs_words, xs_scales, w1, w2_words, w2_scales, b1, gain, w3, w4_words, w4_scales, out
):
    nc = tc.nc
    with ExitStack() as ctx:
        keep = ctx.enter_context(tc.tile_pool(name="keep", bufs=1))
        late = ctx.enter_context(tc.tile_pool(name="late", bufs=1))
        psum = ctx.enter_context(tc.psum_pool(name="psum", bufs=1))

        def tile(name, shape, dtype):
            return keep.tile([P] + shape, dtype, name=name, align_bytes=64)

        def placed(name, shape, dtype, offset):
            return late.tile([P] + shape, dtype, name=name, align_bytes=64, offset=offset)

        def bank(name, index):
            return psum.tile([P, BANK], F32, name=name, tag="bank%d" % index)

        def load_plane(plane, rows):
            for r in range(LIVE):
                nc.sync.dma_start(out=plane[r:P:QUADRANT].bitcast(I32), in_=rows[r:BLOCKS:LIVE].bitcast(I32))

        bias_at = 4 * T
        gains_at = bias_at + 64
        w4_codes_at = gains_at + 64
        w4_plane_at = w4_codes_at + 4 * N
        w1_at = w4_plane_at + 2 * N
        tab_rows_at = bias_at - 1024

        offsets = keep.tile([P, S // 16], U16, name="offsets")
        xs_plane = tile("xs_plane", [S], U8)
        tab_rows = placed("tab_rows", [T], U8, tab_rows_at)
        v_plane = [tile("v_plane%d" % a, [S], U8) for a in range(K // PASS)]
        w2_plane_raw = tile("w2_plane_raw", [H], U8)
        nc.gpsimd.memset(xs_plane[:].bitcast(I32), 0)
        for zeroed in [tab_rows, w2_plane_raw] + v_plane:
            nc.vector.memset(zeroed[:].bitcast(I32), 0)

        w3_raw = tile("w3_raw", [PACK, N], F32)
        xs_codes = tile("xs_codes", [S], I32)
        w2_raw = tile("w2_raw", [2 * H], U8)
        tab_codes = [tile("tab_codes0", [T], I32), placed("tab_codes1", [T], I32, 0)]

        def load_table_half(a, half):
            cols = slice(half * T // 2, (half + 1) * T // 2)
            words = tab_words[a].rearrange("p c i -> p (c i)").bitcast(I32)
            nc.sync.dma_start(out=tab_codes[a][:, cols], in_=words[:, cols])

        load_plane(xs_plane, xs_scales[0])
        nc.sync.dma_start(out=w3_raw[:], in_=w3.rearrange("(p i) n -> p i n", i=PACK))
        nc.sync.dma_start(out=xs_codes[:], in_=xs_words[0].rearrange("p c i -> p (c i)").bitcast(I32))
        nc.sync.dma_start(out=tab_rows[0:P:SPREAD].bitcast(I32), in_=tab_scales.rearrange("a q c -> (a q) c").bitcast(I32))
        nc.sync.dma_start(offsets[:], offs)
        load_table_half(0, 0)
        nc.sync.dma_start(out=w2_raw[:].bitcast(I32), in_=w2_words[0].bitcast(I32))
        load_plane(w2_plane_raw, w2_scales[0])
        load_table_half(0, 1)

        w3_bf = tile("w3_bf", [N * PACK], BF16)
        nc.vector.tensor_copy(
            out=w3_bf[:].rearrange("p (c u i) -> p c i u", u=RUN, i=PACK),
            in_=w3_raw[:].rearrange("p i (c u) -> p c i u", u=RUN),
        )
        w3_codes = tile("w3_codes", [N], U32)
        w3_plane = tile("w3_plane", [N], U8)
        for lo, hi in ((0, P), (P, N)):
            nc.vector.quantize_mx(
                out=w3_codes[:, lo:hi].bitcast(FP8X4), scales=w3_plane[:, lo:hi], in_=w3_bf[:, PACK * lo : PACK * hi]
            )
        skip_abs = []
        for nt in range(N // P):
            skip_abs.append(tile("skip_abs%d" % nt, [S], F32))
            for jh in range(S // BANK):
                skip = bank("skip%d%d" % (nt, jh), 2 * nt + jh)
                cols = slice(jh * BANK, (jh + 1) * BANK)
                nc.tensor.matmul_mx(
                    out=skip[:],
                    lhsT=w3_codes[:, nt * P : (nt + 1) * P].bitcast(FP8X4),
                    lhsT_scale=w3_plane[:, nt * P : (nt + 1) * P],
                    rhs=xs_codes[:, cols].bitcast(FP8X4),
                    rhs_scale=xs_plane[:, cols],
                    start=True,
                    stop=True,
                )
                nc.scalar.activation(skip_abs[nt][:, cols], skip[:], ACT.Abs)
        damp = []
        for nt in range(N // P):
            root = tile("root%d" % nt, [S], F32)
            nc.scalar.activation(root[:], skip_abs[nt][:], ACT.Abs_reciprocal_sqrt, bias=1.0)
            damp.append(tile("damp%d" % nt, [S], F32))
            nc.scalar.activation(damp[nt][:], root[:], ACT.Square)

        v_rows = tile("v_rows", [S], U8)
        nc.vector.tensor_copy(v_rows[:], tab_rows[:].indirect(offsets[:]))

        def move_scale_rows(a):
            first = SPREAD * BLOCKS * a
            for r in range(LIVE):
                nc.sync.dma_start(
                    out=v_plane[a][r:P:QUADRANT].bitcast(I32),
                    in_=v_rows[first + SPREAD * r : first + SPREAD * BLOCKS : SPREAD * LIVE].bitcast(I32),
                )

        bias = placed("bias", [H // PASS, PACK], F32, bias_at)
        gains = placed("gains", [H // PASS, PACK], F32, gains_at)
        w4_codes = placed("w4_codes", [H // PASS, 2 * N], U8, w4_codes_at)
        w4_plane = placed("w4_plane", [H // PASS, N], U8, w4_plane_at)
        w1_all = placed("w1_all", [K * H // P], F32, w1_at)
        nc.vector.memset(w4_plane[:].rearrange("p b n -> p (b n)").bitcast(I32), 0)
        w1_raw = {}

        def load_w1(b, a):
            at = PACK * PASS * (2 * b + a)
            w1_raw[b, a] = w1_all[:, at : at + PACK * PASS].rearrange("p (i c) -> p i c", i=PACK)
            rows = w1[a * PASS : (a + 1) * PASS, b * PASS : (b + 1) * PASS]
            nc.sync.dma_start(out=w1_raw[b, a], in_=rows.rearrange("(p i) c -> p i c", i=PACK))

        move_scale_rows(0)
        load_w1(0, 0)
        load_table_half(1, 0)
        load_table_half(1, 1)
        load_w1(0, 1)
        move_scale_rows(1)
        nc.sync.dma_start(out=bias[:], in_=b1.rearrange("(b p t) -> p b t", p=P, t=PACK))
        nc.sync.dma_start(out=gains[:], in_=gain.rearrange("(b p t) -> p b t", p=P, t=PACK))
        load_w1(1, 0)
        load_w1(1, 1)
        nc.sync.dma_start(out=w4_codes[:].bitcast(I32), in_=w4_words.rearrange("b p c -> p b c").bitcast(I32))
        load_plane(w4_plane, w4_scales.rearrange("b q n -> q b n"))

        w2_codes = tile("w2_codes", [2 * H], U8)
        nc.vector.tensor_copy(
            out=w2_codes[:].bitcast(U16).rearrange("p (b t m) -> p b t m", t=PACK, m=P),
            in_=w2_raw[:].bitcast(U16).rearrange("p (b m t) -> p b t m", t=PACK, m=P),
        )
        w2_plane = tile("w2_plane", [H], U8)
        nc.vector.tensor_copy(
            out=w2_plane[:].rearrange("p (b t m) -> p b t m", t=PACK, m=P),
            in_=w2_plane_raw[:].rearrange("p (b m t) -> p b t m", t=PACK, m=P),
        )

        v_codes = [tile("v_codes%d" % a, [S], U32) for a in range(K // PASS)]

        def gather_words(a):
            nc.vector.tensor_copy(v_codes[a][:], tab_codes[a][:].bitcast(U32).indirect(offsets[:]))

        gather_words(0)

        w1_bf, w1_codes, w1_plane = {}, {}, {}
        for b in range(H // PASS):
            for a in range(K // PASS):
                w1_bf[b, a] = tile("w1_bf%d%d" % (b, a), [PASS * PACK], BF16)
                w1_codes[b, a] = tile("w1_codes%d%d" % (b, a), [PASS], U32)
                w1_plane[b, a] = tile("w1_plane%d%d" % (b, a), [PASS], U8)

        def cast_w1(b, a, engine_copy, ts=slice(0, PACK), ms=slice(0, P)):
            engine_copy(
                out=w1_bf[b, a][:].rearrange("p (t m i) -> p m i t", t=PACK, i=PACK)[:, ms, :, ts],
                in_=w1_raw[b, a].rearrange("p i (m t) -> p m i t", t=PACK)[:, ms, :, ts],
            )

        def quantize_w1(b, a, first=0, last=PACK):
            cols = slice(first * P, last * P)
            nc.vector.quantize_mx(
                out=w1_codes[b, a][:, cols].bitcast(FP8X4),
                scales=w1_plane[b, a][:, cols],
                in_=w1_bf[b, a][:, PACK * first * P : PACK * last * P],
            )

        pre = {}

        def open_banks(b, jh):
            for t in range(PACK):
                pre[b, jh, t] = bank("pre%d%d%d" % (b, jh, t), PACK * jh + t)

        def probe_pass(b, jh, start):
            cols = slice(jh * BANK, (jh + 1) * BANK)
            for t in range(PACK):
                first = b * PASS + t * P
                nc.tensor.matmul_mx(
                    out=pre[b, jh, t][:],
                    lhsT=w2_codes[:, 2 * first : 2 * (first + P)].bitcast(FP4X4),
                    lhsT_scale=w2_plane[:, first : first + P],
                    rhs=xs_codes[:, cols].bitcast(FP8X4),
                    rhs_scale=xs_plane[:, cols],
                    start=start,
                    stop=False,
                )

        def table_pass(b, jh, a, start=False):
            cols = slice(jh * BANK, (jh + 1) * BANK)
            for t in range(PACK):
                nc.tensor.matmul_mx(
                    out=pre[b, jh, t][:],
                    lhsT=w1_codes[b, a][:, t * P : (t + 1) * P].bitcast(FP8X4),
                    lhsT_scale=w1_plane[b, a][:, t * P : (t + 1) * P],
                    rhs=v_codes[a][:, cols].bitcast(FP8X4),
                    rhs_scale=v_plane[a][:, cols],
                    start=start,
                    stop=(a == K // PASS - 1),
                )

        act, h_bf, h_codes, h_plane = {}, {}, {}, {}

        def silu(b, jh):
            for half in range(BANK // HALF):
                act[b, jh, half] = tile("act%d%d%d" % (b, jh, half), [PACK, HALF], F32)
                for t in range(PACK):
                    nc.scalar.activation(
                        act[b, jh, half][:, t, :],
                        pre[b, jh, t][:, half * HALF : (half + 1) * HALF],
                        ACT.Silu,
                        bias=bias[:, b, t : t + 1],
                    )

        def apply_gain(b, jh, half):
            h_bf[b, jh, half] = tile("h_bf%d%d%d" % (b, jh, half), [HALF * PACK], BF16)
            nc.vector.tensor_tensor(
                out=h_bf[b, jh, half][:].rearrange("p (c u t) -> p c t u", u=RUN, t=PACK),
                in0=act[b, jh, half][:].rearrange("p t (c u) -> p c t u", u=RUN),
                in1=gains[:, b : b + 1, :].unsqueeze(3).to_broadcast([P, HALF // RUN, PACK, RUN]),
                op=MULT,
            )

        def quantize_h(b, jh, half):
            if half == 0:
                h_codes[b, jh] = tile("h_codes%d%d" % (b, jh), [BANK], U32)
                h_plane[b, jh] = tile("h_plane%d%d" % (b, jh), [BANK], U8)
            cols = slice(half * HALF, (half + 1) * HALF)
            nc.vector.quantize_mx(
                out=h_codes[b, jh][:, cols].bitcast(FP8X4), scales=h_plane[b, jh][:, cols], in_=h_bf[b, jh, half][:]
            )

        scores = {}

        def score_pass(jh, b):
            for nt in range(N // P):
                if b == 0:
                    scores[jh, nt] = bank("score%d%d" % (jh, nt), PACK * jh + nt)
                nc.tensor.matmul_mx(
                    out=scores[jh, nt][:],
                    lhsT=w4_codes[:, b, 2 * nt * P : 2 * (nt + 1) * P].bitcast(FP4X4),
                    lhsT_scale=w4_plane[:, b, nt * P : (nt + 1) * P],
                    rhs=h_codes[b, jh][:].bitcast(FP8X4),
                    rhs_scale=h_plane[b, jh][:],
                    start=(b == 0),
                    stop=(b == H // PASS - 1),
                )

        def finish(jh, nt, first, width):
            cols = slice(jh * BANK + first, jh * BANK + first + width)
            result = tile("result%d%d_%d" % (jh, nt, first), [width], F32)
            nc.vector.tensor_tensor(
                out=result[:], in0=scores[jh, nt][:, first : first + width], in1=damp[nt][:, cols], op=MULT
            )
            nc.sync.dma_start(out=out[nt * P : (nt + 1) * P, cols], in_=result[:])

        cast_w1(0, 0, nc.vector.tensor_copy)
        quantize_w1(0, 0)
        for jh in range(S // BANK):
            open_banks(0, jh)
            table_pass(0, jh, 0, start=True)
        for jh in range(S // BANK):
            probe_pass(0, jh, False)
        gather_words(1)
        for first in (0, 2):
            cast_w1(0, 1, nc.vector.tensor_copy, ts=slice(first, first + 2))
            quantize_w1(0, 1, first, first + 1)
            quantize_w1(0, 1, first + 1, first + 2)
        table_pass(0, 0, 1)
        table_pass(0, 1, 1)
        silu(0, 0)
        silu(0, 1)

        cast_w1(1, 1, nc.scalar.copy, ms=slice(0, P // 2))
        cast_w1(1, 0, nc.vector.tensor_copy)
        apply_gain(0, 0, 0)
        quantize_w1(1, 0)
        apply_gain(0, 0, 1)
        cast_w1(1, 1, nc.vector.tensor_copy, ms=slice(P // 2, P))
        quantize_h(0, 0, 0)
        for jh in range(S // BANK):
            open_banks(1, jh)
            probe_pass(1, jh, True)
            table_pass(1, jh, 0)
        quantize_w1(1, 1)
        table_pass(1, 0, 1)
        table_pass(1, 1, 1)
        silu(1, 0)
        silu(1, 1)

        steps = [(0, 0, 1)] + [(b, jh, half) for b, jh in ((0, 1), (1, 0), (1, 1)) for half in range(BANK // HALF)]
        for i in range(1, len(steps)):
            apply_gain(*steps[i])
            quantize_h(*steps[i - 1])
        quantize_h(*steps[-1])

        for jh in range(S // BANK):
            for b in range(H // PASS):
                score_pass(jh, b)
        tiles = [(jh, nt) for jh in range(S // BANK) for nt in range(N // P)]
        for jh, nt in tiles[:-1]:
            finish(jh, nt, 0, BANK)
        for first in (0, HALF):
            finish(*tiles[-1], first, HALF)
